import numpy as np, ml_dtypes
CORES = [16,17,18,19,32,33,34,35]
N = 8
BF = ml_dtypes.bfloat16
def gentries(a):
    return np.ascontiguousarray(a.reshape(8, 16, -1).transpose(0, 2, 1)).reshape(8, -1)
def gtable(e):
    e = np.asarray(e); return np.ascontiguousarray(e.reshape(8, -1, 16).transpose(0, 2, 1)).reshape(128, -1).astype(np.int32)
S, C, B, U, RO, Q = 4096, 2048, 128, 64, 3, 8
L = B + U
def parts(rng):
    sk = (256 * (0.25 + 0.75 * rng.random((N, 8, 1, C))) * rng.random((N, 8, 16, C))).astype(np.int64); sk = np.minimum(sk, 255); sk[..., C - 1] = 0
    oc = np.where(rng.random((N, 8, S)) < 0.05, C - 1, rng.integers(0, C - 1, (N, 8, S)))
    cv = rng.integers(0, S, (N, 8, 16, S)); cd = np.ascontiguousarray(np.argsort(rng.random((N, 8, RO, S)), axis=-1)[..., :L * 16])
    return sk, oc, cv, cd
def fill(rng, share):
    u = rng.random((N, 8, 1, RO, B)); v = rng.random((N, 8, 1, RO, B))
    h = np.where(u < share, 9 + 31 * v, np.where(u < share + 0.1, 4 + 5 * v, np.where(u < share + 0.3, 0.0, 0.2 + 3.8 * v)))
    w = rng.random((N, 8, 16, RO, B)) * (rng.random((N, 8, 16, RO, B)) < 0.7)
    return np.minimum((80 * h * w).astype(np.int64), 4096)
def sums(sk, oc, cd):
    who = np.take_along_axis(oc, cd[:, :, 0, :B * 16], 2)
    return np.add.accumulate(np.take_along_axis(sk, who[:, :, None, :], 3).reshape(N, 8, 16, B, 16), axis=4)
def heavy(rng, sk, oc, cv, cd, nd):
    own = np.arange(S); j = np.arange(B)
    for g in rng.permutation(8)[:2]:
        left = []
        for q in range(N):
            v = rng.integers(200, 256, (16, C)); v[:, C - 1] = 0; e = rng.integers(L, C - 1, S)
            st = cd[q, g, 0].reshape(L, 16); late = st[B:].reshape(-1)
            cd[q, g, 1] = np.concatenate([rng.permutation(st[:B].reshape(-1)), rng.permutation(late)])
            cv[q, g] = rng.choice(np.setdiff1d(own, late), (16, S))
            p = rng.integers(10, 16, B); before = np.add.accumulate(v[:, e[st[:B]]], axis=2)[:, j, p - 1]
            x = 208 + (-before) % 16; want = before + x
            x[rng.integers(0, 16, B), j] -= rng.integers(0, 2, B)
            v[:, :B] = x; e[st[j, p]] = j
            big = rng.permutation(B)[:U // 2]; e[st[big[U // 8:], 8:]] = C - 1
            want[:, big] = 0; want[rng.integers(0, 16, U // 2), big] = 4096
            sk[q, g] = v; oc[q, g] = e; nd[q, g] = 0; nd[q, g, :, 0] = want
            end = np.add.reduce(v[:, e[st[:B]]], axis=2); u = np.nonzero(np.any(end < want, axis=0))[0][:U]
            left.append(np.maximum(want[:, u] - end[:, u], 0))
        for q in range(N):
            w = left[q - 1]; n = w.shape[1]; k = np.arange(n); z = np.argmax(w, axis=0); top = w[z, k]
            st = cd[q, g, 1].reshape(L, 16)[B:B + n]
            line = np.add.accumulate(sk[q, g][z[:, None], oc[q, g][st]], axis=1)
            p = np.add.reduce((line < top[:, None]).astype(np.int64), axis=1)
            before = np.where(p > 0, line[k, np.maximum(p - 1, 0)], 0)
            sk[q, g, z, B + k] = top - before - k % 2; oc[q, g, st[k, p]] = B + k
def pack(sk, oc, cv, cd, nd):
    return {"skill": np.ascontiguousarray(sk.reshape(N, 128, C)).astype(np.float32).astype(BF), "occ": oc.astype(np.int32), "cover": np.ascontiguousarray(cv.reshape(N, 128, S)).astype(np.int32),
            "cards": np.stack([gtable(a.reshape(8, -1)) for a in cd]), "need": np.ascontiguousarray(nd.reshape(N, 128, RO * B)).astype(np.float32).astype(BF)}
def setup_inputs(rng):
    sk, oc, cv, cd = parts(rng)
    return pack(sk, oc, cv, cd, fill(rng, rng.choice(np.array([0.03, 0.1, 0.2, 0.3]), (N, 8, 1, 1, 1))))
def setup_inputs_room(rng):
    sk, oc, cv, cd = parts(rng); nd = np.zeros((N, 8, 16, RO, B), np.int64); pre = sums(sk, oc, cd)
    nd[:, :, :, 0] = pre[..., 0] * (rng.random((N, 8, 1, B)) < 0.5)
    for q in range(N):
        for t in range(RO):
            size = rng.permutation(np.array([0, 1, U - 1, U, U + 1, B, U, 0]))
            for g in range(8):
                n = int(size[g]); lanes = rng.permutation(B)[:n]
                nd[q, g, :, t, lanes] = rng.integers(0, 256, (n, 16)); nd[q, g, rng.integers(0, 16, n), t, lanes] = 4096
    return pack(sk, oc, cv, cd, nd)
def setup_inputs_ties(rng):
    sk, oc, cv, cd = parts(rng)
    few = rng.integers(0, 3, sk.shape) * 16; m = np.arange(8)[None, :, None, None] % 2 == 0
    sk = np.where(m, few, sk // 16 * 16) * (rng.random((N, 8, 1, C)) > 0.1); sk[..., C - 1] = 0
    nd = fill(rng, 0.05); pre = sums(sk, oc, cd)
    p = rng.choice(np.array([0, 0, 1, 3, 7, 14, 15, 15]), (N, 8, B))
    w = np.take_along_axis(pre, p[:, :, None, :, None], 4)[..., 0]
    w = w + 16 * ((np.arange(16)[None, None, :, None] == rng.integers(0, 16, (N, 8, 1, B))) & (rng.random((N, 8, 1, B)) < 0.5))
    nd[:, :, :, 0] = w * (rng.random((N, 8, 1, B)) > 0.3)
    heavy(rng, sk, oc, cv, cd, nd)
    return pack(sk, oc, cv, cd, nd)
def setup_inputs_crowd(rng):
    sk, oc, cv, cd = parts(rng); h = B // 2; sk[..., 0] = 255; own = np.arange(S); o = rng.permutation(8)
    full = np.argsort(rng.random((N, 8, B)), axis=-1)[..., :U]
    for q in range(N):
        for g in range(8):
            card = cd[q, g, 0].reshape(L, 16)
            if g == o[0] or g == o[1]:
                k = rng.permutation(np.setdiff1d(own, card[full[q, g]].reshape(-1))); a, b = k[:L], k[L:2 * L]
                mid = rng.permutation(np.setdiff1d(own, k[:2 * L]))[:14 * L].reshape(L, 14)
                cd[q, g, 1] = np.concatenate([a[:, None], mid, b[:, None]], axis=1).reshape(-1)
                v = np.clip(sk[q, g], 16, 239); v[:, :16] = rng.integers(240, 256, (16, 16)); v[:, C - 1] = 0; sk[q, g] = v
                oc[q, g, a] = rng.integers(16, C - 1, L); oc[q, g, b] = rng.integers(0, 16, L)
                c = np.repeat(own[None, :], 16, axis=0)
                if g == o[0]: c[:, a] = b[rng.integers(0, 2, (16, L))]
                else: c[:, a] = np.where(np.arange(16)[:, None] >= rng.integers(0, 16, L)[None, :], b[None, :], a[None, :])
                cv[q, g] = c
            else:
                pool = card[h:h + 16, 15]; oc[q, g, pool[:8]] = 0
                c = pool[rng.integers(0, 16, (16, S))]; kind = rng.integers(0, 5, S)
                c[:15] = np.where(kind >= 3, own, c[:15]); c[15] = np.where(kind == 4, own, c[15]); cv[q, g] = c
    nd = fill(rng, 0.05); pre = sums(sk, oc, cd)
    nd[:, :, :, 0] = pre[..., 0] * (np.arange(B) < h); nd[:, o[:2]] = 0
    for q in range(N):
        for g in o[:2]:
            z = rng.integers(0, 16, U); l = full[q, g]; nd[q, g, z, 0, l] = pre[q, g, z, l, 15] // 16 * 16 + 16
            nd[q, g, rng.integers(0, 16, B), 1, np.arange(B)] = rng.integers(1, 17, B)
    return pack(sk, oc, cv, cd, nd)
def setup_inputs_bare(rng):
    sk, oc, cv, cd = parts(rng); h = rng.permutation(8)
    oc = np.where(rng.random((N, 8, S)) < rng.choice(np.array([0.4, 0.6, 0.8]), (N, 8, 1)), C - 1, oc); oc[:, h[0]] = C - 1
    ends = np.array([0, 1, S - 2, S - 1]); cv[:, h[2]] = rng.choice(ends, (N, 16, S)); oc[:, h[2], :2] = rng.integers(0, C - 1, (N, 2)); oc[:, h[2], S - 2:] = rng.integers(0, C - 1, (N, 2))
    nd = fill(rng, 0.05) * (rng.random((N, 8, 1, RO, B)) < 0.5); nd[::2, h[1]] = 0
    return pack(sk, oc, cv, cd, nd)
def setup_inputs_spread(rng):
    sk, oc, cv, cd = parts(rng)
    sk = np.minimum((np.exp2(8.2 * rng.random((N, 8, 1, C))) * rng.random((N, 8, 16, C))).astype(np.int64), 255); sk[..., C - 1] = 0
    oc = np.where(rng.random((N, 8, S)) < 0.1, C - 1, np.minimum(((C - 1) * rng.random((N, 8, S)) ** 3).astype(np.int64), C - 2))
    cv = np.minimum((S * rng.random((N, 8, 16, S)) ** 2).astype(np.int64), S - 1)
    nd = (np.minimum(np.exp2(12.2 * rng.random((N, 8, 1, RO, B))), 4096) * rng.choice(np.array([0.0, 0.25, 0.5, 1.0]), (N, 8, 16, RO, B))).astype(np.int64)
    return pack(sk, oc, cv, cd, nd * (rng.random((N, 8, 1, RO, B)) > 0.3))
def check_inputs(d):
    bad = []
    for k, hi in (("skill", 255), ("need", 4096), ("occ", C - 1), ("cover", S - 1), ("cards", S - 1)):
        x = np.asarray(d[k]).astype(np.float64)
        if not np.all((x >= 0) & (x <= hi) & (x == np.floor(x))): bad.append("range of " + k)
    if not np.all(np.asarray(d["skill"])[:, :, C - 1].astype(np.float32) == 0): bad.append("last column of skill")
    e = np.sort(np.asarray(d["cards"]).reshape(N, 8, 16, RO, L).transpose(0, 1, 3, 2, 4).reshape(N, 8, RO, 16 * L), axis=-1)
    if np.any(e[..., 1:] == e[..., :-1]): bad.append("equal stations on the cards of a round")
    return bad
def reference(skill, occ, cover, cards, need):
    sk = skill.astype(np.float32).astype(np.int64).reshape(N, 8, 16, C); cv = cover.astype(np.int64).reshape(N, 8, 16, S)
    cd = np.stack([gentries(a) for a in cards]).astype(np.int64).reshape(N, 8, RO, L, 16); nd = need.astype(np.float32).astype(np.int64).reshape(N, 8, 16, RO, B)
    oc = np.array(occ, dtype=np.int64); arrived = np.zeros((N, 8, 16, U), np.int64)
    for t in range(RO):
        sent = np.zeros((N, 8, 16, U), np.int64)
        for r in range(N):
            w = np.concatenate([nd[r, :, :, t], arrived[r]], axis=2)
            st = cd[r, :, t]; flat = st.reshape(8, -1)
            who = np.take_along_axis(oc[r], flat, 1)
            col = np.take_along_axis(sk[r], who[:, None, :], 2).reshape(8, 16, L, 16)
            pre = np.add.accumulate(col, axis=3)
            met = np.all(pre >= w[..., None], axis=1)
            zero = np.all(w == 0, axis=1)
            leave = ~np.concatenate([zero[..., None], met[..., :15]], axis=2)
            unmet = ~met[..., 15]; before = np.add.accumulate(unmet.astype(np.int64), axis=1) - unmet
            rest = np.maximum(w - pre[..., 15], 0); g, l = np.nonzero(unmet & (before < U))
            sent[(r + 1) % N][g, :, before[g, l]] = rest[g, :, l]
            np.put_along_axis(oc[r], flat, np.where(leave.reshape(8, -1), C - 1, who), 1)
            s = st[..., 0]; lost = leave[..., 0] & (who.reshape(8, L, 16)[..., 0] != C - 1)
            m = np.take_along_axis(cv[r], s[:, None, :], 2)
            a = np.take_along_axis(oc[r], m.reshape(8, -1), 1)
            ka = np.take_along_axis(sk[r], a[:, None, :], 2).reshape(8, 16, 16, L)
            a = a.reshape(8, 16, L); good = np.add.reduce((ka >= col[:, :, None, :, 0]).astype(np.int64), axis=1)
            fit = (a != C - 1) & (good >= Q); ok = lost & np.any(fit, axis=1)
            i = np.argmax(fit, axis=1)[:, None, :]
            src = np.take_along_axis(m, i, 1)[:, 0]; new = np.take_along_axis(a, i, 1)[:, 0]
            for g in range(8):
                lanes = np.nonzero(ok[g])[0]
                out, at = np.unique(src[g, lanes], return_index=True); lanes = lanes[at]
                oc[r, g, s[g, lanes]] = new[g, lanes]; oc[r, g, out] = C - 1
        arrived = sent
    return {"y": oc.astype(np.float32)}

from concourse.mybir import dt, AluOpType as A_, ActivationFunctionType as F_

EPS = 2.0 ** -40
BIGS = 8192.0
NST, NDUMP, NWIN = 4096, 4480, 4496
KV = 12

TYPES = {"b": "bfloat16", "f": "float32", "i": "int32", "u": "uint16", "h": "float16"}
BUFS = """b skw 2048  i occ32 256  f occf 256  u bof 256  b skp 4096  b SK 8960  f NUM 8960  i cov 4096  i cd32 576
i cs32 576  u cu 576  u cm 576  h ch 576  b nd 384  b XA 2064  b XB 1040  b a15 64  b N1 2048  f N2 1024  b R1 2048  b R2 1024
b keep 3072  b AG 3072  b ge 3072  f mf 192  f ms 192  u mu 192  h code16 192  b eb 192  b bsb 192  b Fb 192  b sel 192
h selm 192  h Rh 192  f vx 192  f tg 12  f offf 12  f tu 12  f slf 12  u LL0 16  u LL1 24  u LL2 24  b sv0 256  b sv1 384
f nv 384  b um 192  f us 192  f uf 192  b ux 192  b cum 192  f uy 192  u ul 12  f df 192  f SW0 384  f SW1 384  f RC0 64
f RC1 64  u L0u 72  f L0f 36  i pmi 1  i pmj 1  f pmf 1  f pk 1  f pz 1  f th0 1  f thr 1  i ia 192  i ic 192  i ib 192
f dtf 192  f duf 192  f DT 192  f DU 192  b OD 192  b TC 192  b ones 160  b OB 160  b OBa 160  b OB8 128  b OBn 128
h OBh 128  b Wb 160  h Wh 160  b Zb 160  h Zh 160  b Yb 160  h Yh 160  b Ib 128  b I5 128  b In 128  b Tri 128  b T8 128
b EL 256  f NL 256  f ef 256  f YL 256""".split()
SCRATCH = {BUFS[k + 1]: ("sbuf", [128, int(BUFS[k + 2])], TYPES[BUFS[k]]) for k in range(0, len(BUFS), 3)}
SCRATCH["E2"] = ("sbuf", [128, 12, 192], "bfloat16")
SCRATCH["PL"] = ("psum", [128, 3072], "float32")
SCRATCH["PM"] = ("psum", [128, 512], "float32")
SCRATCH["PN"] = ("psum", [128, 512], "float32")
SEMAPHORES = ["qV", "qS", "qP", "qG", "arr0", "arr1", "snt"] + ["d%d" % i for i in range(14)]


def tracker(g, T):
    eng = {"V": g.vector, "S": g.scalar, "P": g.tensor, "G": g, "Y": g.sync}
    num = {"V": 0, "S": 0, "P": 0, "G": 0, "D": 0}
    know = {q: {} for q in eng}
    snaps, lastw, readers = {}, {}, {}

    def semof(p):
        return T.sem["q" + p] if p in "VSPG" else T.sem[p]

    def waits(q, deps):
        best = {}
        for p, n in deps:
            if know[q].get(p, 0) < n:
                best[p] = max(n, best.get(p, 0))
        items = list(best.items())
        for p, n in items:
            if any(p2 != p and snaps[(p2, n2)].get(p, 0) >= n for p2, n2 in items):
                continue
            eng[q].wait_ge(semof(p), n)
        k = know[q]
        for p, n in items:
            for a, b in snaps[(p, n)].items():
                k[a] = max(k.get(a, 0), b)
            k[p] = max(k.get(p, 0), n)

    def before(q, R, W):
        d = [lastw[r] for r in R if r in lastw]
        for r in R:
            if r[:2] in ("PL", "PM", "PN"):
                d += [x for x in readers.get(r, []) if x[0] != q]
        for w in W:
            if w in lastw and not (q == "P" and lastw[w][0] == "P"):
                d.append(lastw[w])
            d += readers.get(w, [])
        waits(q, d)

    def note(tok, R, W):
        for r in R:
            readers.setdefault(r, []).append(tok)
        for w in W:
            lastw[w] = tok
            readers[w] = []

    def op(q, fns, R, W):
        before(q, R, W)
        fns = fns if isinstance(fns, list) else [fns]
        for f in fns[:-1]:
            f()
        num[q] += 1
        fns[-1]().then_inc(semof(q), 1)
        tok = (q, num[q])
        snaps[tok] = dict(know[q])
        note(tok, R, W)

    def dma(q, out, in_, R, W):
        before(q, R, W)
        p = "d%d" % num["D"]
        num["D"] += 1
        eng[q].dma_start(out, in_).then_inc(T.sem[p], 16)
        tok = (p, 16)
        snaps[tok] = dict(know[q])
        note(tok, R, W)

    def arrive(p, n, W):
        snaps[(p, n)] = {}
        note((p, n), [], W)

    def finish():
        for p, n in [(q, num[q]) for q in "VSPG" if num[q]] + [("d%d" % i, 16) for i in range(num["D"])]:
            if know["G"].get(p, 0) < n:
                g.wait_ge(semof(p), n)

    return op, dma, arrive, before, finish


def rank_program(g, core, T, topo):
    rank = T.rank_of(core)
    if rank is None:
        return
    cores = list(T.cores)
    nxt = cores[(rank + 1) % len(cores)]
    NE = 4
    V, S, P = g.vector, g.scalar, g.tensor
    op, dma, arrive, before, finish = tracker(g, T)
    arrive("arr0", NE, ["RC0"])
    arrive("arr1", NE, ["RC1"])
    SKW = ["SK", "SKd"] + ["SK_%d" % i for i in range(16)]
    RD = SKW + ["SKb"]

    def v(fn, R, W):
        op("V", fn, R, W)

    def s(fn, R, W):
        op("S", fn, R, W)

    def p(fns, R, W):
        op("P", fns, R, W)

    def gp(fn, R, W):
        op("G", fn, R, W)

    def mm(out, l, r, a, b):
        return lambda: P.matmul(out, l, r, a, b)

    dma("Y", T.occ32[:, :], T.occ[:, :], [], ["occ32"])
    dma("S", T.cs32[1:128, :], T.cards[0:127, :], [], ["cs32a"])
    dma("Y", T.skw[:, :], T.skill[:, :], [], ["skw"])
    dma("S", T.cs32[0:1, :], T.cards[127:128, :], [], ["cs32b"])
    dma("S", T.cd32[:, :], T.cards[:, :], [], ["cd32"])
    dma("S", T.nd[:, :], T.need[:, :], [], ["nd"])
    dma("Y", T.cov[:, :], T.cover[:, :], [], ["cov"])

    v(lambda: V.memset(T.ones[:, :], 1.0), [], ["ones"])
    gp(lambda: g.iota(T.pmi[:, :], [[0, 1]], 0, 1), [], ["pmi"])
    gp(lambda: g.iota(T.ib[:, :], [[16, 12], [0, 16]], 4097, 0), [], ["ib"])
    gp(lambda: g.iota(T.ia[:, :], [[1, 192]], 256, -1), [], ["ia"])
    gp(lambda: g.affine_select(T.OBa[:, :], T.ones[:, :], [[-16, 10], [0, 16]], A_.is_ge, 0.0, 16, 1), ["ones"], ["OBa"])
    gp(lambda: g.affine_select(T.OB[:, :], T.OBa[:, :], [[16, 10], [0, 16]], A_.is_ge, 0.0, -1, -1), ["OBa"], ["OB"])
    gp(lambda: g.affine_select(T.Wb[:, :], T.OB[:, :], [[0, 10], [1, 16]], A_.is_equal, 0.0, 0, 0), ["OB"], ["Wb"])
    gp(lambda: g.affine_select(T.Zb[:, :], T.Wb[:, :], [[1, 160]], A_.is_equal, 0.0, -16, -1), ["Wb"], ["Zb"])
    gp(lambda: g.affine_select(T.Yb[:, :], T.Wb[:, :], [[1, 160]], A_.is_equal, 0.0, -1, -1), ["Wb"], ["Yb"])
    gp(lambda: g.affine_select(T.Ib[:, :], T.ones[:, 0:128], [[1, 128]], A_.is_equal, 0.0, 0, -1), ["ones"], ["Ib"])
    gp(lambda: g.affine_select(T.Tri[:, :], T.OB[:, 16:144], [[1, 128]], A_.is_gt, 0.0, 0, -1), ["OB"], ["Tri"])
    v(lambda: V.memset(T.SK[:, NST:NDUMP], 0.0), [], ["SKd"])
    v(lambda: V.memset(T.SK[:, NDUMP:NWIN], BIGS), [], ["SKb"])
    v(lambda: V.memset(T.N1[:, :], 0.0), [], ["N1"])
    v(lambda: V.tensor_scalar(T.pmj[:, :], T.pmi[:, :], 15, None, A_.bitwise_and), ["pmi"], ["pmj"])
    v(lambda: V.memset(T.N2[:, :], 0.0), [], ["N2"])
    v(lambda: V.tensor_copy(T.pmf[:, :], T.pmj[:, :]), ["pmj"], ["pmf"])
    v(lambda: V.tensor_scalar(T.ic[:, :], T.ia[:, :], 15, None, A_.bitwise_and), ["ia"], ["ic"])
    v(lambda: V.tensor_scalar(T.pk[:, :], T.pmf[:, :], 0.0, None, A_.is_gt), ["pmf"], ["pk"])
    v(lambda: V.tensor_scalar(T.pz[:, :], T.pmf[:, :], 0.0, float(NDUMP), A_.is_equal, A_.mult), ["pmf"], ["pz"])
    v(lambda: V.tensor_scalar(T.th0[:, :], T.pmf[:, :], float(KV), 8.0, A_.is_lt, A_.mult), ["pmf"], ["th0"])
    v(lambda: V.tensor_copy(T.bof[:, :], T.occ32[:, :]), ["occ32"], ["bof"])
    v(lambda: V.tensor_scalar(T.cm[:, 0:192], T.cs32[:, 0:192], T.pk[:, 0:1], T.pz[:, 0:1], A_.mult, A_.add), ["cs32a", "cs32b", "pk", "pz"], ["cm0"])
    v(lambda: V.tensor_scalar(T.dtf[:, :], T.ib[:, :], T.pmf[:, 0:1], None, A_.add), ["ib", "pmf"], ["dtf"])
    v(lambda: V.tensor_scalar(T.OD[:, :], T.ic[:, :], 0.0, BIGS, A_.not_equal, A_.mult), ["ic"], ["OD"])
    v(lambda: V.tensor_scalar(T.thr[:, :], T.th0[:, :], -0.5, None, A_.add), ["th0"], ["thr"])
    v(lambda: V.tensor_scalar(T.duf[:, :], T.dtf[:, :], -3905.0, None, A_.add), ["dtf"], ["duf"])
    v(lambda: V.tensor_copy(T.Wh[:, :], T.Wb[:, :]), ["Wb"], ["Wh"])
    v(lambda: V.tensor_scalar(T.TC[:, :], T.OD[:, :], 10240.0, None, A_.add), ["OD"], ["TC"])
    v(lambda: V.memset(T.SW0[:, 0:64], 0.0), [], ["SW0"])
    v(lambda: V.memset(T.SW1[:, 0:64], 0.0), [], ["SW1"])
    gp(lambda: g.affine_select(T.DT[:, :], T.dtf[:, :], [[0, 12], [1, 16]], A_.is_equal, 0.0, 0, 0), ["dtf"], ["DT"])
    gp(lambda: g.affine_select(T.DU[:, :], T.duf[:, :], [[0, 12], [1, 16]], A_.is_equal, 0.0, 0, 0), ["duf"], ["DU"])
    gp(lambda: g.iota(T.NUM[:, 0:NDUMP], [[0, NDUMP]], 0, 0, allow_small_or_imprecise_dtypes=True), [], ["NUM"])
    v(lambda: V.memset(T.skw[:, 2047:2048], -1.0), [], ["skw"])
    v(lambda: V.tensor_scalar(T.skp[:, 0:2048], T.skw[:, :].indirect(T.bof[:, 0:128]), EPS, 0.0, A_.add, A_.max), ["skw", "bof"], ["skpa"])
    s(lambda: S.activation(T.skp[:, 2048:4096], T.skw[:, :].indirect(T.bof[:, 128:256]), F_.Relu, bias=EPS), ["skw", "bof"], ["skpb"])
    v(lambda: V.tensor_scalar(T.N1[:, 0:2048:16], T.nd[:, 0:128], -1.0, None, A_.mult), ["nd"], ["N1"])
    v(lambda: V.tensor_scalar(T.ch[:, :], T.cd32[:, :], -2048.0, None, A_.add), ["cd32"], ["ch"])
    v(lambda: V.tensor_copy(T.Zh[:, :], T.Zb[:, :]), ["Zb"], ["Zh"])
    v(lambda: V.tensor_copy(T.Yh[:, :], T.Yb[:, :]), ["Yb"], ["Yh"])
    p([mm(T.PN[:, 0:36], T.Zh[:, 16 - i:144 - i], T.ch[:, i:576:16], i == 0, i == 15) for i in range(16)], ["Zh", "ch"], ["PN"])
    p([mm(T.PN[:, 36:72], T.Yh[:, 16 - i:144 - i], T.ch[:, i:576:16], i == 0, i == 15) for i in range(16)], ["Yh", "ch"], ["PN"])
    for i in range(16):
        if i < 10:
            v(lambda: V.tensor_copy(T.SK[:, 256 * i:256 * i + 256], T.skp[:, i:4096:16]), ["skpa", "skpb"], ["SK_%d" % i])
        else:
            s(lambda: S.activation(T.SK[:, 256 * i:256 * i + 256], T.skp[:, i:4096:16], F_.Copy), ["skpa", "skpb"], ["SK_%d" % i])
    v(lambda: V.tensor_scalar(T.L0u[:, :], T.PN[:, 0:72], 2048.0, None, A_.add), ["PN"], ["L0u"])

    def prep_m(t):
        L = 128 if t == 0 else 192
        v(lambda: V.tensor_copy(T.mf[:, 0:L], T.cov[:, :].indirect(T.L0u[:, 12 * t:12 * t + L // 16])), ["cov", "L0u"], ["mf"])
        v(lambda: V.tensor_copy(T.mu[:, 0:L], T.mf[:, 0:L]), ["mf"], ["mu"])

    def prep_s(t):
        L = 128 if t == 0 else 192
        s(lambda: S.activation(T.ms[:, 0:L], T.mf[:, 0:L], F_.Sign, bias=-2047.5), ["mf"], ["ms"])
        s(lambda: S.activation(T.PN[:, 256:256 + L], T.ms[:, 0:L], F_.Copy, bias=-2047.5, scale=0.5), ["ms"], ["PN"])

    def prep_c(t):
        L = 128 if t == 0 else 192
        v(lambda: V.tensor_tensor(T.code16[:, 0:L], T.mf[:, 0:L], T.PN[:, 256:256 + L], A_.add), ["mf", "PN"], ["code16"])

    win = T.SK[:, 0:NWIN]

    for t in range(3):
        last = t == 2
        L = 128 if t == 0 else 192
        C = L // 16
        H = L // 2
        c0 = 192 * t
        LL = T["LL%d" % t]
        sv = T.sv0 if t == 0 else T.sv1
        kv = "0" if t == 0 else "1"
        cuk, cmk = (["cu0"], ["cm0"]) if t == 0 else (["cu1"], ["cm1"])

        def leave(b, src, key):
            p(mm(T.PL[:, 512 * b:512 * b + 512], T.OB[:, 16:144], src, True, True), ["OB", key], ["PL%d" % b])

        def scat(k):
            src = T.XA[:, 1 + 1024 * k:1025 + 1024 * k] if k < 2 else T.XB[:, 1:1025]
            v(lambda: V.tensor_tensor(win.indirect(T.cu[:, c0 + 64 * k:c0 + 64 * k + 64]), src, T.keep[:, 1024 * k:1024 * k + 1024], A_.mult),
              cuk + ["keep%d" % k] + (["XA0", "XA1", "XAf"] if k < 2 else ["XBa", "XBb", "XBf"]), SKW)

        v(lambda: V.tensor_copy(T.XA[:, 0:1024], win.indirect(T.cm[:, c0:c0 + 64])), RD + cmk, ["XA0"])
        s(lambda: S.activation(T.XA[:, 1024:2048], win.indirect(T.cm[:, c0 + 64:c0 + 128]), F_.Copy), RD + cmk, ["XA1"])
        if t:
            s(lambda: S.activation(T.XB[:, 512:1024], win.indirect(T.cm[:, c0 + 160:c0 + 192]), F_.Copy), RD + cmk, ["XBb"])
        v(lambda: V.tensor_tensor_scan(T.R1[:, 0:1024], T.XA[:, 0:1024], T.N1[:, 0:1024], 0.0, A_.add, A_.min), ["XA0", "XAf", "N1"], ["R1a"])
        for b in range(2):
            leave(b, T.R1[:, 512 * b:512 * b + 512], "R1a")
        if t:
            v(lambda: V.tensor_copy(T.XB[:, 0:512], win.indirect(T.cm[:, c0 + 128:c0 + 160])), RD + cmk, ["XBa"])
        s(lambda: S.activation(T.keep[:, 0:1024], T.PL[:, 0:1024], F_.Relu, bias=1.0), ["PL0", "PL1"], ["keep0"])
        if t:
            v(lambda: V.tensor_copy(T.a15[:, 0:64], win.indirect(T.L0u[:, 44 + 12 * t:48 + 12 * t])), RD + ["L0u"], ["a15"])
        v(lambda: V.tensor_tensor_scan(T.R1[:, 1024:2048], T.XA[:, 1024:2048], T.N1[:, 1024:2048], 0.0, A_.add, A_.min), ["XA1", "XAf", "N1"], ["R1b"])
        for b in range(2, 4):
            leave(b, T.R1[:, 512 * b:512 * b + 512], "R1b")
        s(lambda: S.activation(T.keep[:, 1024:2048], T.PL[:, 1024:2048], F_.Relu, bias=1.0), ["PL2", "PL3"], ["keep1"])
        v(lambda: V.tensor_copy(T.XA[:, 16:2064:16], win.indirect(T.L0u[:, 36 + 12 * t:44 + 12 * t])), RD + ["L0u", "XA0", "XA1"], ["XAf"])
        if t == 0:
            v(lambda: V.tensor_copy(T.cu[:, 0:192], T.cd32[:, 0:192]), ["cd32"], ["cu0"])
            v(lambda: V.tensor_scalar(T.L0f[:, :], T.PN[:, 0:36], 2048.0, None, A_.add), ["PN"], ["L0f"])
            v(lambda: V.tensor_copy(T.occf[:, :], T.occ32[:, :]), ["occ32"], ["occf"])
            dma("Y", T.NUM[0:128:16, 0:NST], T.occf[:, :], ["occf"], ["NUM"])
        else:
            prep_c(t)
        scat(0)
        if t == 0:
            prep_m(0)
            s(lambda: S.activation(T.I5[:, :], T.Ib[:, :], F_.Copy, scale=512.0), ["Ib"], ["I5"])
            s(lambda: S.activation(T.In[:, :], T.Ib[:, :], F_.Copy, scale=-1.0), ["Ib"], ["In"])
        else:
            rc = T["RC%d" % (t - 1)]
            v(lambda: V.tensor_scalar(T.N2[:, 0:1024:16], rc[:, :], 0.0, None, A_.min), ["RC%d" % (t - 1)], ["N2"])
            v(lambda: V.tensor_tensor_scan(T.R2[:, :], T.XB[:, 0:1024], T.N2[:, :], 0.0, A_.add, A_.min), ["XBa", "XBb", "XBf", "N2"], ["R2"])
            for b in range(4, 6):
                leave(b, T.R2[:, 512 * (b - 4):512 * (b - 4) + 512], "R2")
            s(lambda: S.activation(T.keep[:, 2048:3072], T.PL[:, 2048:3072], F_.Relu, bias=1.0), ["PL4", "PL5"], ["keep2"])
            v(lambda: V.tensor_copy(T.XB[:, 16:1040:16], T.a15[:, :]), ["a15", "XBa", "XBb"], ["XBf"])
        if not last:
            p([mm(T.PN[:, 0:128], T.Ib[:, :], T.XA[:, 1 + i:2048:16], i == 0, False) for i in range(15)]
              + [mm(T.PN[:, 0:128], T.Ib[:, :], T.XA[:, 16:2064:16], False, False), mm(T.PN[:, 0:128], T.In[:, :], T.nd[:, 128 * t:128 * t + 128], False, True)],
              ["Ib", "In", "nd", "XA0", "XA1", "XAf"], ["PN"])
            if t:
                p([mm(T.PN[:, 128:192], T.Ib[:, :], T.XB[:, 1 + i:1024:16], i == 0, False) for i in range(15)]
                  + [mm(T.PN[:, 128:192], T.Ib[:, :], T.a15[:, :], False, True)], ["Ib", "XBa", "XBb", "a15"], ["PN"])
        s(lambda: S.activation(T.eb[:, 0:128], T.XA[:, 1:2048:16], F_.Relu, bias=512.0, scale=-(2.0 ** 50)), ["XA0", "XA1"], ["eb"])
        p([mm(T.PL[:, 0:128], T.Ib[:, :], T.XA[:, 1:2048:16], True, False), mm(T.PL[:, 0:128], T.I5[:, :], T.keep[:, 0:2048:16], False, False),
           mm(T.PL[:, 0:128], T.Ib[:, :], T.eb[:, 0:128], False, True)], ["Ib", "I5", "XA0", "XA1", "keep0", "keep1", "eb"], ["PL0"])
        scat(1)
        if t and not last:
            v(lambda: V.tensor_tensor(T.df[:, 128:192], T.PN[:, 128:192], T.N2[:, 0:1024:16], A_.add), ["PN", "N2"], ["dfb"])
        if t:
            scat(2)
            s(lambda: S.activation(T.eb[:, 128:192], T.XB[:, 1:1024:16], F_.Relu, bias=512.0, scale=-(2.0 ** 50)), ["XBa", "XBb"], ["eb"])
            p([mm(T.PL[:, 128:192], T.Ib[:, :], T.XB[:, 1:1024:16], True, False), mm(T.PL[:, 128:192], T.I5[:, :], T.keep[:, 2048:3072:16], False, False),
               mm(T.PL[:, 128:192], T.Ib[:, :], T.eb[:, 128:192], False, True)], ["Ib", "I5", "XBa", "XBb", "keep2", "eb"], ["PL0"])
        s(lambda: S.activation(T.bsb[:, 0:L], T.PL[:, 0:L], F_.Copy), ["PL0"], ["bsb"])
        if not last:
            s(lambda: S.activation(T.df[:, 0:128], T.PN[:, 0:128], F_.Copy), ["PN"], ["df"])
            s(lambda: S.activation(T.um[:, 0:L], T.df[:, 0:L], F_.Relu, scale=-1.0), ["df", "dfb"], ["um"])
            p(mm(T.PM[:, 0:L], T.OB[:, 16:144], T.um[:, 0:L], True, True), ["OB", "um"], ["PM"])
            s(lambda: S.activation(T.us[:, 0:L], T.PM[:, 0:L], F_.Sign, bias=-0.5), ["PM"], ["us"])
            s(lambda: S.activation(T.uf[:, 0:L], T.us[:, 0:L], F_.Relu), ["us"], ["uf"])
            s(lambda: S.activation(T.ux[:, 0:L], T.uf[:, 0:L], F_.Copy, bias=8191.0, scale=-8192.0), ["uf"], ["ux"])
            s(lambda: S.activation(T.N1[:, 0:2048:16], T.nd[:, 128 * t + 128:128 * t + 256], F_.Copy, scale=-1.0), ["nd"], ["N1"])
        if t == 0:
            s(lambda: S.activation(T.OB8[:, :], T.OB[:, 16:144], F_.Copy, scale=8192.0), ["OB"], ["OB8"])
            s(lambda: S.activation(T.OBn[:, :], T.OB[:, 16:144], F_.Copy, scale=-8192.0), ["OB"], ["OBn"])
            s(lambda: S.activation(T.T8[:, :], T.Tri[:, :], F_.Copy, scale=8192.0), ["Tri"], ["T8"])
            prep_s(0)
        v(lambda: V.tensor_copy(T.AG[:, 0:16 * H], win.indirect(T.mu[:, 0:H])), RD + ["mu"], ["AGa"])
        s(lambda: S.activation(T.AG[:, 16 * H:16 * L], win.indirect(T.mu[:, H:L]), F_.Copy), RD + ["mu"], ["AGb"])
        if last:
            dma("Y", T.EL[:, :], T.SK[0:128:16, 0:NST], SKW, ["EL"])
        for i in range(KV):
            v(lambda: V.tensor_tensor(T.ge[:, L * i:L * i + L], T.AG[:, i:16 * L:16], T.PL[:, 0:L], A_.is_ge), ["AGa", "AGb", "PL0"], ["ge%d" % i])
        order = list(range(4))
        for k in range((16 - KV) // 2):
            b = 512 * (2 + k)
            i = KV + 2 * k
            for h in range(2):
                p([mm(T.PL[:, b + L * h:b + L * h + L], T.Ib[:, :], T.AG[:, i + h:16 * L:16], True, False),
                   mm(T.PL[:, b + L * h:b + L * h + L], T.In[:, :], T.bsb[:, 0:L], False, True)], ["Ib", "In", "AGa", "AGb", "bsb"], ["PL%d" % (2 + k)])
            s(lambda: S.activation(T.ge[:, L * i:L * i + 2 * L], T.PL[:, b:b + 2 * L], F_.Sign, bias=EPS / 2), ["PL%d" % (2 + k)], ["ge%d" % i, "ge%d" % (i + 1)])
            order += [i, i + 1]
            order += list(range(4 + 2 * k, min(6 + 2 * k, KV)))
        order += [i for i in range(16) if i not in order]
        for i in order:
            p(mm(T.PL[:, 512:512 + L], T.Wb[:, 16 - i:144 - i], T.ge[:, L * i:L * i + L], i == order[0], i == order[-1]), ["Wb", "ge%d" % i], ["PL1"] if i in (order[0], order[-1]) else [])
        if t == 0:
            prep_c(0)
            v(lambda: V.tensor_copy(T.OBh[:, :], T.OB[:, 16:144]), ["OB"], ["OBh"])
        if not last:
            v(lambda: V.tensor_tensor_scan(T.cum[:, 0:L], T.uf[:, 0:L], T.uf[:, 0:L], 0.0, A_.add, A_.max), ["uf"], ["cum"])
            prep_m(t + 1)
        v(lambda: V.tensor_scalar(T.Fb[:, 0:L], T.PL[:, 512:512 + L], T.thr[:, 0:1], None, A_.is_ge), ["PL1", "thr"], ["Fb"])
        p(mm(T.PL[:, 1024:1024 + L], T.Tri[:, :], T.Fb[:, 0:L], True, True), ["Tri", "Fb"], ["PL2"])
        if not last:
            p([mm(T.PM[:, 0:L], T.Ib[:, :], T.OD[:, 0:L], True, False), mm(T.PM[:, 0:L], T.Ib[:, :], T.ux[:, 0:L], False, False),
               mm(T.PM[:, 0:L], T.Ib[:, :], T.cum[:, 0:L], False, True)], ["Ib", "OD", "ux", "cum"], ["PM"])
        else:
            v(lambda: V.tensor_scalar(T.ef[:, :], T.EL[:, :], 0.0, 2047.0, A_.is_equal, A_.mult), ["EL"], ["ef"])
        v(lambda: V.tensor_tensor(T.sel[:, 0:L], T.PL[:, 1024:1024 + L], T.Fb[:, 0:L], A_.is_lt), ["PL2", "Fb"], ["sel"])
        v(lambda: V.tensor_tensor(T.selm[:, 0:L], T.sel[:, 0:L], T.code16[:, 0:L], A_.mult), ["sel", "code16"], ["selm"])
        p(mm(T.PL[:, 1536:1536 + L], T.OBh[:, :], T.selm[:, 0:L], True, True), ["OBh", "selm"], ["PL3"])
        p([mm(T.PL[:, 2048:2048 + C], T.Wh[:, 16 - i:144 - i], T.selm[:, i:L:16], i == 0, i == 15) for i in range(16)], ["Wh", "selm"], ["PL4"])
        if not last:
            sw = T["SW%d" % t]
            v(lambda: V.tensor_tensor_scan(T.uy[:, 0:L], T.DU[:, 0:L], T.PM[:, 0:L], 0.0, A_.max, A_.min), ["DU", "PM"], ["uy"])
            v(lambda: V.tensor_copy(T.ul[:, 0:C], T.uy[:, 15:L:16]), ["uy"], ["ul"])
            v(lambda: V.tensor_copy(sw[:, :].indirect(T.ul[:, 0:C]), T.df[:, 0:L]), ["ul", "df", "dfb"], ["SW%d" % t])
            before("G", ["SW%d" % t], [])
            rid, pid, _se = topo.addr(nxt)
            em = sum(1 << e for e in topo.engines(core, nxt)[:NE])
            g.remote_dma(T["RC%d" % t][:, :], sw[:, 0:64], T.sem["arr%d" % t], T.sem.snt, pid, rid, em)
        else:
            v(lambda: V.tensor_tensor(T.YL[:, :], T.NL[:, :], T.ef[:, :], A_.max), ["NL", "ef"], ["YL"])
            dma("Y", T.NUM[0:128:16, 0:NST], T.YL[:, :], ["YL"], ["NUM"])
        v(lambda: V.tensor_copy(T.Rh[:, 0:L], T.PL[:, 1536:1536 + L]), ["PL3"], ["Rh"])
        for c in range(C):
            v(lambda: V.tensor_scalar(T.E2[:, c, 0:L - 16 * c], T.Rh[:, 16 * c:L], T.PL[:, 2048 + c:2049 + c], None, A_.is_equal), ["Rh", "PL4"], ["E%d" % c])
        X = T.PL[:, 2560:2560 + L]
        p([mm(X, T.Ib[:, :], T.TC[:, 0:L], True, False), mm(X, T.OBh[:, :], T.selm[:, 0:L], False, False),
           mm(X, T.OBn[:, :], T.sel[:, 0:L], False, False)], ["Ib", "TC", "OBh", "selm", "OBn", "sel"], ["PL5"])
        for c in range(C - 1):
            p(mm(T.PL[:, 2560 + 16 * c + 16:2560 + L], T.OB8[:, :], T.E2[:, c, 16:L - 16 * c], False, False), ["OB8", "E%d" % c], [])
        p(mm(X, T.T8[:, :], T.E2[:, 0:C, 0:16], False, True), ["T8"] + ["E%d" % c for c in range(C)], ["PL5"])
        if not last:
            prep_s(t + 1)
        v(lambda: V.tensor_tensor_scan(T.vx[:, 0:L], T.DT[:, 0:L], X, 0.0, A_.max, A_.min), ["DT", "PL5"], ["vx"])
        v(lambda: V.tensor_scalar(T.tg[:, 0:C], T.vx[:, 15:L:16], 2048.0, -1.0, A_.is_gt, A_.mult), ["vx"], ["tg"])
        v(lambda: V.tensor_tensor(T.offf[:, 0:C], T.vx[:, 15:L:16], T.tg[:, 0:C], A_.add), ["vx", "tg"], ["offf"])
        v(lambda: V.tensor_copy(LL[:, C:2 * C], T.offf[:, 0:C]), ["offf"], ["LLb"])
        if not last:
            s(lambda: S.activation(sv[:, 0:L], win.indirect(LL[:, C:2 * C]), F_.Copy), RD + ["LLb"], ["sv" + kv])
        s(lambda: S.activation(T.nv[:, 0:L], T.NUM[:, 0:NDUMP].indirect(LL[:, C:2 * C]), F_.Copy), ["NUM", "LLb"], ["nv"])
        v(lambda: V.tensor_scalar(T.tu[:, 0:C], T.vx[:, 15:L:16], 4096.5, float(NWIN), A_.is_gt, A_.mult), ["vx"], ["tu"])
        v(lambda: V.tensor_tensor(T.slf[:, 0:C], T.tu[:, 0:C], T.L0f[:, 12 * t:12 * t + C], A_.add), ["tu", "L0f"], ["slf"])
        v(lambda: V.tensor_copy(LL[:, 0:C], T.slf[:, 0:C]), ["slf"], ["LLa"])
        if t == 0:
            v(lambda: V.memset(T.sv0[:, 128:256], 0.0), [], ["sv0z"])
        if not last:
            v(lambda: V.tensor_copy(T.SK[:, :].indirect(LL[:, 0:2 * C]), sv[:, 0:2 * L]), ["LLa", "LLb", "sv" + kv, "sv%sz" % kv], SKW)
        if t == 0:
            v(lambda: V.tensor_scalar(T.cm[:, 192:576], T.cs32[:, 192:576], T.pk[:, 0:1], T.pz[:, 0:1], A_.mult, A_.add), ["cs32a", "cs32b", "pk", "pz"], ["cm1"])
            v(lambda: V.tensor_copy(T.cu[:, 192:576], T.cd32[:, 192:576]), ["cd32"], ["cu1"])
            v(lambda: V.memset(T.sv1[:, 192:384], 0.0), [], ["sv1z"])
            v(lambda: V.memset(T.nv[:, 192:384], 2047.0), [], ["nvz"])
        K = 2 if last else 1
        v(lambda: V.tensor_copy(T.NUM[:, :].indirect(LL[:, 0:K * C]), T.nv[:, 0:K * L]), ["LLa", "LLb", "nv", "nvz"], ["NUM"])
        if t == 1:
            dma("Y", T.NL[:, :], T.NUM[0:128:16, 0:NST], ["NUM"], ["NL"])
    dma("Y", T.y[:, :], T.NUM[0:128:16, 0:NST], ["NUM"], ["y"])
    g.wait_ge(T.sem.snt, 2 * NE)
    finish()
